import numpy as np
import ml_dtypes


def mxq(x, axis, fmt="e4m3"):
    dtype, down = {"e4m3": (ml_dtypes.float8_e4m3fn, 7), "e5m2": (ml_dtypes.float8_e5m2, 14)}[fmt]
    v = np.moveaxis(np.asarray(x, np.float32).astype(ml_dtypes.bfloat16).astype(np.float64), axis, -1)
    blocks = v.reshape(v.shape[:-1] + (-1, 32))
    amax = np.abs(blocks).max(-1, keepdims=True)
    byte = np.maximum(np.where(amax > 0, np.frexp(amax)[1] - 1 + 127, 0) - down, 1)
    scale = np.exp2(byte - 127.0)
    codes = (blocks / scale).astype(np.float32).astype(dtype).astype(np.float64)
    return np.moveaxis((codes * scale).reshape(v.shape), -1, axis)


WIDE = False


def mx_kscale(k):
    if not WIDE:
        return np.ones(k)
    levels = np.array([30, -30])
    if k % 512:
        return np.exp2(np.random.permutation(np.resize(levels, k // 32))).repeat(32)
    a = np.empty((k // 512, 16))
    for p in range(k // 512):
        a[p, :8] = np.random.permutation(np.resize(levels, 8))
        for g in range(8):
            far = levels[np.abs(levels - a[p, g]) >= 10]
            a[p, g + 8] = far[np.random.randint(len(far))]
    return np.exp2(a.ravel()).repeat(32)


def f64(x):
    return np.asarray(x).astype(np.float64)


def striped(idx):
    return np.tile(np.asarray(idx).reshape(-1, 16).T, (8, 1)).astype(np.uint16)


def unstriped(offs):
    return offs[:16].T.reshape(-1).astype(np.int64)


def striped8(idx):
    return np.asarray(idx).reshape(8, -1, 16).transpose(0, 2, 1).reshape(128, -1).astype(np.uint16)


def unstriped8(offs):
    return offs.reshape(8, 16, -1).transpose(0, 2, 1).reshape(8, -1).astype(np.int64)


def pick8(x, idx, run):
    r = np.arange(len(x))
    return x[r[:, None], idx[r % (8 * run) // run]]


E2M1 = np.array([0.0, 0.5, 1.0, 1.5, 2.0, 3.0, 4.0, 6.0, -0.0, -0.5, -1.0, -1.5, -2.0, -3.0, -4.0, -6.0])


def pack_weight(w, fmt):
    k, n = w.shape
    w = f64(np.asarray(w, np.float32).astype(ml_dtypes.bfloat16)).reshape(k // 32, 32, n)
    amax = np.abs(w).max(1)
    if fmt in ("e4m3", "e5m2"):
        byte = np.frexp(amax)[1] - 1 + 127 - (7 if fmt == "e4m3" else 14)
    else:
        mant, ex = np.frexp(amax / 6.0)
        byte = np.where(mant > 0.5, ex, ex - 1) + 127
    byte = np.clip(np.where(amax > 0, byte, 1), 1, 254)
    scaled = (w * np.exp2(127.0 - byte)[:, None, :]).reshape(k, n).astype(np.float32)
    by_word = np.ascontiguousarray(scaled.reshape(k // 512, 128, 4, n).transpose(0, 1, 3, 2))
    if fmt in ("e4m3", "e5m2"):
        words = by_word.astype(ml_dtypes.float8_e4m3fn if fmt == "e4m3" else ml_dtypes.float8_e5m2).view(np.uint8)
    else:
        c = by_word.astype(ml_dtypes.float4_e2m1fn).view(np.uint8) & 0xF
        words = (c[..., 0::2] | (c[..., 1::2] << 4)).reshape(k // 512, 128, 2 * n)
    return np.ascontiguousarray(words), np.ascontiguousarray(byte.astype(np.uint8).reshape(k // 512, 16, n))


def unpack_weight(words, scales, fmt):
    g, _, n = scales.shape
    words = np.ascontiguousarray(words).reshape(g, 128, n, -1)
    if fmt in ("e4m3", "e5m2"):
        vals = words.view(ml_dtypes.float8_e4m3fn if fmt == "e4m3" else ml_dtypes.float8_e5m2).astype(np.float64)
    else:
        nib = np.empty((g, 128, n, 4), np.uint8)
        nib[..., 0::2] = words & 0xF
        nib[..., 1::2] = words >> 4
        vals = E2M1[nib]
    vals = vals * np.repeat(np.exp2(scales.astype(np.float64) - 127.0), 8, axis=1)[..., None]
    return vals.transpose(0, 1, 3, 2).reshape(g * 512, n)


K, T, J, R, C, O, N, E = 512, 1024, 256, 512, 512, 128, 256, 512


def setup_inputs():
    n = np.random.standard_normal
    idx = np.random.permutation(T)[:J]
    idx2 = np.stack([np.random.permutation(C)[:J] for _ in range(8)])
    idx3 = np.stack([np.random.permutation(C)[:J] for _ in range(8)])
    idx4 = np.random.permutation(C)[:O]
    idx5 = np.random.permutation(C)[:O]
    idx6 = np.stack([np.random.permutation(E)[:O] for _ in range(8)])
    idx7 = np.random.permutation(E)[:O]
    fk = mx_kscale(K)
    fr = mx_kscale(R)
    xtp = pack_weight(n((K, T)) / fk[:, None], "e5m2")
    wp = pack_weight(n((K, R)) * 1 / np.sqrt(K) * fk[:, None] * fr, "e2m1")
    w2p = pack_weight(n((K, R)) * 1 / np.sqrt(K) * fk[:, None] * fr, "e4m3")
    wbp = pack_weight(n((R, N)) * 1 / np.sqrt(R) / fr[:, None], "e2m1")
    return {
        "xt_words": xtp[0],
        "xt_scales": xtp[1],
        "w_words": wp[0],
        "w_scales": wp[1],
        "w2_words": w2p[0],
        "w2_scales": w2p[1],
        "sa": (np.random.uniform(0.5, 1.6, (R, 1))).astype(np.float32),
        "sb": (np.random.uniform(0.5, 1.6, (R, 1))).astype(np.float32),
        "wb_words": wbp[0],
        "wb_scales": wbp[1],
        "offs": striped(idx),
        "offs2": striped8(idx2),
        "offs3": striped8(idx3),
        "offs4": striped(idx4),
        "offs5": striped(idx5),
        "offs6": striped8(idx6),
        "offs7": striped(idx7),
    }


def reference(xt_words, xt_scales, w_words, w_scales, w2_words, w2_scales, sa, sb, wb_words, wb_scales, offs, offs2, offs3, offs4, offs5, offs6, offs7):
    idx = unstriped(offs)
    idx2 = unstriped8(offs2)
    idx3 = unstriped8(offs3)
    idx4 = unstriped(offs4)
    idx5 = unstriped(offs5)
    idx6 = unstriped8(offs6)
    idx7 = unstriped(offs7)
    xtu = unpack_weight(xt_words, xt_scales, "e5m2")
    wu = unpack_weight(w_words, w_scales, "e2m1")
    w2u = unpack_weight(w2_words, w2_scales, "e4m3")
    wbu = unpack_weight(wb_words, wb_scales, "e2m1")
    xtidxg = xtu[:, idx]
    a = wu.T @ xtidxg
    b = w2u.T @ xtidxg
    pw = np.zeros((R, C))
    pw[np.arange(R)[:, None], idx2[np.arange(R) % 512 // 64]] = a
    pv = np.zeros((R, C))
    pv[np.arange(R)[:, None], idx3[np.arange(R) % 512 // 64]] = b
    pg = pw + pv
    hid = np.abs(pg[:, idx4] * f64(sa) - pg[:, idx5] * f64(sb))
    hidq = mxq(hid, 0, "e4m3")
    p = wbu.T @ hidq
    pa = np.zeros((N, E))
    pa[np.arange(N)[:, None], idx6[np.arange(N) % 128 // 16]] = p
    pb = np.zeros((N, E))
    pb[:, idx7] = p
    y = pa + pb
    return y

@@ -1,0 +1,179 @@
+from contextlib import ExitStack
+
+import concourse.mybir as mybir
+
+F32 = mybir.dt.float32
+BF16 = mybir.dt.bfloat16
+I32 = mybir.dt.int32
+U32 = mybir.dt.uint32
+U16 = mybir.dt.uint16
+U8 = mybir.dt.uint8
+E4M3X4 = mybir.dt.float8_e4m3fn_x4
+E5M2X4 = mybir.dt.float8_e5m2_x4
+E2M1X4 = mybir.dt.float4_e2m1fn_x4
+COPY = mybir.ActivationFunctionType.Copy
+ALU = mybir.AluOpType
+
+K, T, J, R, C, O, N, E = 512, 1024, 256, 512, 512, 128, 256, 512
+P = 128
+PACK = 4
+QUADS = 4
+QUAD = 32
+FLOPS = 2 * K * R * J * 2 + 2 * R * N * O
+
+
+def tile_list_ownsum_twow_one_owntwopages_kernel(
+    tc, xt_words, xt_scales, w_words, w_scales, w2_words, w2_scales, sa, sb, wb_words, wb_scales,
+    offs, offs2, offs3, offs4, offs5, offs6, offs7, out,
+):
+    nc = tc.nc
+    with ExitStack() as ctx:
+        lists = ctx.enter_context(tc.tile_pool(name="lists", bufs=1))
+        keep = ctx.enter_context(tc.tile_pool(name="keep", bufs=1))
+        psum = ctx.enter_context(tc.psum_pool(name="psum", bufs=1))
+
+        def load_list(src, name):
+            t = lists.tile(list(src.shape), U16, name=name)
+            nc.sync.dma_start(t[:], src)
+            return t
+
+        def load_plane(queue, plane, scales):
+            rows = scales[0].bitcast(I32)
+            for q in range(QUADS):
+                queue.dma_start(plane[QUAD * q : QUAD * q + PACK, :].bitcast(I32), rows[PACK * q : PACK * (q + 1), :])
+
+        def load_staged(queue, scales, name):
+            staged = keep.tile([PACK, QUADS, R // 4], I32, name=name)
+            queue.dma_start(staged[:], scales[0].bitcast(I32).rearrange("(q r) n -> r q n", r=PACK))
+            return staged
+
+        def deal_scales(staged, plane, name):
+            for q in range(QUADS):
+                nc.vector.tensor_copy(plane[QUAD * q : QUAD * q + PACK, :].bitcast(I32), staged[:, q, :])
+            dealt = keep.tile([P, PACK, P], U8, name=name, align_bytes=64)
+            nc.vector.tensor_copy(dealt[:], plane[:].rearrange("p (m t) -> p t m", t=PACK))
+            return dealt
+
+        x_plane = keep.tile([P, T], U8, name="x_plane")
+        nc.vector.memset(x_plane[:].bitcast(I32), 0)
+        w_plane = keep.tile([P, R], U8, name="w_plane")
+        nc.vector.memset(w_plane[:].bitcast(I32), 0)
+        w2_plane = keep.tile([P, R], U8, name="w2_plane")
+        nc.vector.memset(w2_plane[:].bitcast(I32), 0)
+        wb_plane = keep.tile([P, N], U8, name="wb_plane", align_bytes=64)
+        nc.vector.memset(wb_plane[:].bitcast(I32), 0)
+
+        x_table = keep.tile([P, T], I32, name="x_table")
+        w_raw = keep.tile([P, 2 * R], U8, name="w_raw")
+        o1 = load_list(offs, "o1")
+        load_plane(nc.scalar, x_plane, xt_scales)
+        w_staged = load_staged(nc.sync, w_scales, "w_staged")
+        nc.sync.dma_start(w_raw[:].bitcast(I32), w_words[0].bitcast(I32))
+        nc.sync.dma_start(x_table[:], xt_words[0].rearrange("p n t -> p (n t)").bitcast(I32))
+        o2 = load_list(offs2, "o2")
+        w2_staged = load_staged(nc.sync, w2_scales, "w2_staged")
+        w2_raw = keep.tile([P, R], I32, name="w2_raw")
+        nc.sync.dma_start(w2_raw[:], w2_words[0].rearrange("p n t -> p (n t)").bitcast(I32))
+        o3 = load_list(offs3, "o3")
+        o4 = load_list(offs4, "o4")
+        o5 = load_list(offs5, "o5")
+        sa_t = keep.tile([P, PACK], F32, name="sa_t")
+        nc.sync.dma_start(sa_t[:], sa.rearrange("(p t) o -> p (t o)", t=PACK))
+        sb_t = keep.tile([P, PACK], F32, name="sb_t")
+        nc.sync.dma_start(sb_t[:], sb.rearrange("(p t) o -> p (t o)", t=PACK))
+        wb_t = keep.tile([P, 2 * N], U8, name="wb_t", align_bytes=64)
+        nc.sync.dma_start(wb_t[:].bitcast(I32), wb_words[0].bitcast(I32))
+        load_plane(nc.sync, wb_plane, wb_scales)
+        o6 = load_list(offs6, "o6")
+        o7 = load_list(offs7, "o7")
+
+        boards = {}
+        for side in ("pw", "pv"):
+            for half in range(2):
+                boards[side, half] = keep.tile([P, C], F32, name="%s%d" % (side, half))
+        for half in range(2):
+            for side in ("pw", "pv"):
+                nc.vector.memset(boards[side, half][:], 0.0)
+
+        w_dealt = keep.tile([P, PACK, 2 * P], U8, name="w_dealt", align_bytes=64)
+        nc.scalar.copy(w_dealt[:].bitcast(U16), w_raw[:].bitcast(U16).rearrange("p (m t) -> p t m", t=PACK))
+        ws_dealt = deal_scales(w_staged, w_plane, "ws_dealt")
+        xs = keep.tile([P, J], U8, name="xs", align_bytes=64)
+        nc.vector.tensor_copy(xs[:], x_plane[:].indirect(o1[:]))
+        xw = keep.tile([P, J], U32, name="xw", align_bytes=64)
+        nc.vector.tensor_copy(xw[:], x_table[:].bitcast(U32).indirect(o1[:]))
+
+        def product(name, words, scales):
+            acc = psum.tile([P, J], F32, name=name + "_acc")
+            nc.tensor.matmul_mx(out=acc[:], lhsT=words, lhsT_scale=scales, rhs=xw[:].bitcast(E5M2X4), rhs_scale=xs[:],
+                                start=True, stop=True)
+            res = keep.tile([P, J], F32, name=name)
+            nc.vector.tensor_copy(res[:], acc[:])
+            return res
+
+        a = [product("a0", w_dealt[:, 0, :].bitcast(E2M1X4), ws_dealt[:, 0, :])]
+        w2s_dealt = deal_scales(w2_staged, w2_plane, "w2s_dealt")
+        w2_dealt = keep.tile([P, PACK, P], I32, name="w2_dealt", align_bytes=64)
+        nc.vector.tensor_copy(w2_dealt[:], w2_raw[:].rearrange("p (m t) -> p t m", t=PACK))
+        b = [product("b0", w2_dealt[:, 0, :].bitcast(E4M3X4), w2s_dealt[:, 0, :])]
+        for t in range(1, PACK):
+            a.append(product("a%d" % t, w_dealt[:, t, :].bitcast(E2M1X4), ws_dealt[:, t, :]))
+            b.append(product("b%d" % t, w2_dealt[:, t, :].bitcast(E4M3X4), w2s_dealt[:, t, :]))
+
+        hid = keep.tile([P, O, PACK], BF16, name="hid", align_bytes=64)
+        pg = {}
+
+        def place(t):
+            pw, pv = boards["pw", t % 2], boards["pv", t % 2]
+            nc.scalar.activation(pw[:].indirect(o2[:]), a[t][:], COPY)
+            nc.scalar.activation(pv[:].indirect(o3[:]), b[t][:], COPY)
+            pg[t] = keep.tile([P, C], F32, name="pg%d" % t)
+            nc.vector.tensor_tensor(pg[t][:], pw[:], pv[:], ALU.add)
+
+        def fetch(t):
+            first = keep.tile([P, O], F32, name="first%d" % t)
+            nc.scalar.activation(first[:], pg[t][:].indirect(o4[:]), COPY, scale=sa_t[:, t : t + 1])
+            second = keep.tile([P, O], F32, name="second%d" % t)
+            nc.scalar.activation(second[:], pg[t][:].indirect(o5[:]), COPY, scale=sb_t[:, t : t + 1])
+            diff = keep.tile([P, O], F32, name="diff%d" % t)
+            nc.vector.tensor_tensor(diff[:], first[:], second[:], ALU.subtract)
+            nc.vector.scalar_tensor_tensor(hid[:, :, t], diff[:], -1.0, diff[:], ALU.mult, ALU.max)
+
+        place(0)
+        place(1)
+        fetch(0)
+        place(2)
+        fetch(1)
+        place(3)
+        fetch(2)
+        fetch(3)
+
+        hq = keep.tile([P, O], U32, name="hq", align_bytes=64)
+        hs = keep.tile([P, O], U8, name="hs", align_bytes=64)
+        nc.vector.quantize_mx(out=hq[:].bitcast(E4M3X4), scales=hs[:], in_=hid[:].rearrange("p o t -> p (o t)"))
+
+        pages = {}
+        for m in range(N // P):
+            for side in ("pa", "pb"):
+                pages[side, m] = keep.tile([P, E], F32, name="%s%d" % (side, m))
+                nc.vector.memset(pages[side, m][:], 0.0)
+
+        res = []
+        for m in range(N // P):
+            acc = psum.tile([P, O], F32, name="p_acc%d" % m, tag="a%d_acc" % m)
+            nc.tensor.matmul_mx(out=acc[:], lhsT=wb_t[:, 2 * P * m : 2 * P * (m + 1)].bitcast(E2M1X4),
+                                lhsT_scale=wb_plane[:, P * m : P * (m + 1)], rhs=hq[:].bitcast(E4M3X4), rhs_scale=hs[:],
+                                start=True, stop=True)
+            p_sb = keep.tile([P, O], F32, name="p%d" % m)
+            if m == 0:
+                nc.vector.tensor_copy(p_sb[:], acc[:])
+            else:
+                nc.scalar.copy(p_sb[:], acc[:])
+            res.append(p_sb)
+        for m in range(N // P):
+            nc.scalar.activation(pages["pa", m][:].indirect(o6[:]), res[m][:], COPY)
+            nc.vector.tensor_copy(pages["pb", m][:].indirect(o7[:]), res[m][:])
+        for m in range(N // P):
+            y = keep.tile([P, E], F32, name="y%d" % m)
+            nc.vector.tensor_tensor(y[:], pages["pa", m][:], pages["pb", m][:], ALU.add)
+            nc.sync.dma_start(out[P * m : P * (m + 1), :], y[:])

@@ -47,29 +47,27 @@ def tile_list_ownsum_twow_one_owntwopages_kernel(
             queue.dma_start(staged[:], scales[0].bitcast(I32).rearrange("(q r) n -> r q n", r=PACK))
             return staged
 
-        def deal_scales(staged, plane, name):
+        def spread_scales(staged, plane):
             for q in range(QUADS):
                 nc.vector.tensor_copy(plane[QUAD * q : QUAD * q + PACK, :].bitcast(I32), staged[:, q, :])
-            dealt = keep.tile([P, PACK, P], U8, name=name, align_bytes=64)
-            nc.vector.tensor_copy(dealt[:], plane[:].rearrange("p (m t) -> p t m", t=PACK))
-            return dealt
 
-        x_plane = keep.tile([P, T], U8, name="x_plane")
+        def dealt_view(ap):
+            return ap.rearrange("p (m t) -> p t m", t=PACK)
+
+        x_plane = keep.tile([P, T], U8, name="x_plane", align_bytes=64)
         nc.vector.memset(x_plane[:].bitcast(I32), 0)
         w_plane = keep.tile([P, R], U8, name="w_plane")
         nc.vector.memset(w_plane[:].bitcast(I32), 0)
-        w2_plane = keep.tile([P, R], U8, name="w2_plane")
-        nc.vector.memset(w2_plane[:].bitcast(I32), 0)
         wb_plane = keep.tile([P, N], U8, name="wb_plane", align_bytes=64)
         nc.vector.memset(wb_plane[:].bitcast(I32), 0)
 
-        x_table = keep.tile([P, T], I32, name="x_table")
+        x_table = keep.tile([P, T], I32, name="x_table", align_bytes=64)
         w_raw = keep.tile([P, 2 * R], U8, name="w_raw")
         o1 = load_list(offs, "o1")
-        load_plane(nc.scalar, x_plane, xt_scales)
         w_staged = load_staged(nc.sync, w_scales, "w_staged")
-        nc.sync.dma_start(w_raw[:].bitcast(I32), w_words[0].bitcast(I32))
+        load_plane(nc.scalar, x_plane, xt_scales)
         nc.sync.dma_start(x_table[:], xt_words[0].rearrange("p n t -> p (n t)").bitcast(I32))
+        nc.sync.dma_start(w_raw[:].bitcast(I32), w_words[0].bitcast(I32))
         o2 = load_list(offs2, "o2")
         w2_staged = load_staged(nc.sync, w2_scales, "w2_staged")
         w2_raw = keep.tile([P, R], I32, name="w2_raw")
@@ -88,44 +86,73 @@ def tile_list_ownsum_twow_one_owntwopages_kernel(
         o7 = load_list(offs7, "o7")
 
         boards = {}
-        for side in ("pw", "pv"):
-            for half in range(2):
-                boards[side, half] = keep.tile([P, C], F32, name="%s%d" % (side, half))
-        for half in range(2):
-            for side in ("pw", "pv"):
-                nc.vector.memset(boards[side, half][:], 0.0)
 
-        w_dealt = keep.tile([P, PACK, 2 * P], U8, name="w_dealt", align_bytes=64)
-        nc.scalar.copy(w_dealt[:].bitcast(U16), w_raw[:].bitcast(U16).rearrange("p (m t) -> p t m", t=PACK))
-        ws_dealt = deal_scales(w_staged, w_plane, "ws_dealt")
+        def clear_board(side, half, tag):
+            boards[side, half] = keep.tile([P, C], F32, name="%s%d" % (side, half), tag=tag, align_bytes=64)
+            nc.vector.memset(boards[side, half][:], 0.0)
+
+        clear_board("pw", 0, "pw0")
+        clear_board("pw", 1, "pw1")
+
+        w_first = keep.tile([P, 2 * P], U8, name="w_first", align_bytes=64)
+        nc.scalar.copy(w_first[:].bitcast(U16), dealt_view(w_raw[:].bitcast(U16))[:, 0, :])
+        w_rest = keep.tile([P, PACK - 1, 2 * P], U8, name="w_rest", align_bytes=64)
+        nc.scalar.copy(w_rest[:].bitcast(U16), dealt_view(w_raw[:].bitcast(U16))[:, 1:, :])
+        spread_scales(w_staged, w_plane)
+        ws_first = keep.tile([P, P], U8, name="ws_first", align_bytes=64)
+        nc.vector.tensor_copy(ws_first[:], dealt_view(w_plane[:])[:, 0, :])
         xs = keep.tile([P, J], U8, name="xs", align_bytes=64)
         nc.vector.tensor_copy(xs[:], x_plane[:].indirect(o1[:]))
-        xw = keep.tile([P, J], U32, name="xw", align_bytes=64)
-        nc.vector.tensor_copy(xw[:], x_table[:].bitcast(U32).indirect(o1[:]))
+        xw = keep.tile([P, J], U32, name="xw", tag="x_plane", align_bytes=64)
+        HALF = J // 2
+        halves = [(slice(HALF * h, HALF * (h + 1)), slice(HALF // 16 * h, HALF // 16 * (h + 1))) for h in range(2)]
+        for cols, offc in halves:
+            nc.vector.tensor_copy(xw[:, cols], x_table[:].bitcast(U32).indirect(o1[:, offc]))
 
-        def product(name, words, scales):
-            acc = psum.tile([P, J], F32, name=name + "_acc")
-            nc.tensor.matmul_mx(out=acc[:], lhsT=words, lhsT_scale=scales, rhs=xw[:].bitcast(E5M2X4), rhs_scale=xs[:],
+        def product(name, words, scales, cols, tag):
+            width = cols.stop - cols.start
+            acc = psum.tile([P, width], F32, name=name + "_acc", tag=tag)
+            nc.tensor.matmul_mx(out=acc[:], lhsT=words, lhsT_scale=scales, rhs=xw[:, cols].bitcast(E5M2X4), rhs_scale=xs[:, cols],
                                 start=True, stop=True)
-            res = keep.tile([P, J], F32, name=name)
+            res = keep.tile([P, width], F32, name=name, align_bytes=64)
             nc.vector.tensor_copy(res[:], acc[:])
             return res
 
-        a = [product("a0", w_dealt[:, 0, :].bitcast(E2M1X4), ws_dealt[:, 0, :])]
-        w2s_dealt = deal_scales(w2_staged, w2_plane, "w2s_dealt")
-        w2_dealt = keep.tile([P, PACK, P], I32, name="w2_dealt", align_bytes=64)
-        nc.vector.tensor_copy(w2_dealt[:], w2_raw[:].rearrange("p (m t) -> p t m", t=PACK))
-        b = [product("b0", w2_dealt[:, 0, :].bitcast(E4M3X4), w2s_dealt[:, 0, :])]
+        whole = slice(0, J)
+        a0 = [product("a0_%d" % h, w_first[:].bitcast(E2M1X4), ws_first[:], halves[h][0], "bank%d" % h) for h in range(2)]
+        ws_rest = keep.tile([P, PACK - 1, P], U8, name="ws_rest", tag="ws_first", align_bytes=64)
+        nc.vector.tensor_copy(ws_rest[:], dealt_view(w_plane[:])[:, 1:, :])
+        a = [None]
         for t in range(1, PACK):
-            a.append(product("a%d" % t, w_dealt[:, t, :].bitcast(E2M1X4), ws_dealt[:, t, :]))
-            b.append(product("b%d" % t, w2_dealt[:, t, :].bitcast(E4M3X4), w2s_dealt[:, t, :]))
+            a.append(product("a%d" % t, w_rest[:, t - 1, :].bitcast(E2M1X4), ws_rest[:, t - 1, :], whole, "bank%d" % (1 + t)))
+        clear_board("pw", 2, "w_first")
+        clear_board("pw", 3, "ws_first")
+        clear_board("pv", 0, "w_rest")
+        w2_plane = keep.tile([P, R], U8, name="w2_plane", tag="w_plane")
+        nc.vector.memset(w2_plane[:].bitcast(I32), 0)
+        spread_scales(w2_staged, w2_plane)
+        w2s_dealt = keep.tile([P, PACK, P], U8, name="w2s_dealt", align_bytes=64)
+        nc.vector.tensor_copy(w2s_dealt[:], dealt_view(w2_plane[:]))
+        w2_dealt = keep.tile([P, PACK, P], I32, name="w2_dealt", tag="a0_0", align_bytes=64)
+        nc.vector.tensor_copy(w2_dealt[:], dealt_view(w2_raw[:]))
+        b = []
+        for t in range(PACK):
+            b.append(product("b%d" % t, w2_dealt[:, t, :].bitcast(E4M3X4), w2s_dealt[:, t, :], whole, "bank%d" % ((5 + t) % 8)))
+        clear_board("pv", 1, "w2s_dealt")
 
         hid = keep.tile([P, O, PACK], BF16, name="hid", align_bytes=64)
         pg = {}
 
-        def place(t):
-            pw, pv = boards["pw", t % 2], boards["pv", t % 2]
-            nc.scalar.activation(pw[:].indirect(o2[:]), a[t][:], COPY)
+        def place_first(t):
+            pw = boards["pw", t]
+            if t == 0:
+                for h in range(2):
+                    nc.scalar.activation(pw[:].indirect(o2[:, halves[h][1]]), a0[h][:], COPY)
+            else:
+                nc.scalar.activation(pw[:].indirect(o2[:]), a[t][:], COPY)
+
+        def place_second(t):
+            pw, pv = boards["pw", t], boards["pv", t % 2]
             nc.scalar.activation(pv[:].indirect(o3[:]), b[t][:], COPY)
             pg[t] = keep.tile([P, C], F32, name="pg%d" % t)
             nc.vector.tensor_tensor(pg[t][:], pw[:], pv[:], ALU.add)
@@ -139,12 +166,23 @@ def tile_list_ownsum_twow_one_owntwopages_kernel(
             nc.vector.tensor_tensor(diff[:], first[:], second[:], ALU.subtract)
             nc.vector.scalar_tensor_tensor(hid[:, :, t], diff[:], -1.0, diff[:], ALU.mult, ALU.max)
 
-        place(0)
-        place(1)
+        pages = {}
+
+        def clear_pages(m, tags):
+            for side, tag in zip(("pa", "pb"), tags):
+                pages[side, m] = keep.tile([P, E], F32, name="%s%d" % (side, m), tag=tag, align_bytes=64)
+                nc.vector.memset(pages[side, m][:], 0.0)
+
+        for t in range(PACK):
+            place_first(t)
+        place_second(0)
+        place_second(1)
+        clear_pages(0, ("pw0", "b0"))
         fetch(0)
-        place(2)
+        place_second(2)
+        clear_pages(1, ("pw1", "b1"))
         fetch(1)
-        place(3)
+        place_second(3)
         fetch(2)
         fetch(3)
 
@@ -152,28 +190,25 @@ def tile_list_ownsum_twow_one_owntwopages_kernel(
         hs = keep.tile([P, O], U8, name="hs", align_bytes=64)
         nc.vector.quantize_mx(out=hq[:].bitcast(E4M3X4), scales=hs[:], in_=hid[:].rearrange("p o t -> p (o t)"))
 
-        pages = {}
-        for m in range(N // P):
-            for side in ("pa", "pb"):
-                pages[side, m] = keep.tile([P, E], F32, name="%s%d" % (side, m))
-                nc.vector.memset(pages[side, m][:], 0.0)
-
         res = []
         for m in range(N // P):
-            acc = psum.tile([P, O], F32, name="p_acc%d" % m, tag="a%d_acc" % m)
+            acc = psum.tile([P, O], F32, name="p_acc%d" % m, tag="bank%d" % (1 + m))
             nc.tensor.matmul_mx(out=acc[:], lhsT=wb_t[:, 2 * P * m : 2 * P * (m + 1)].bitcast(E2M1X4),
                                 lhsT_scale=wb_plane[:, P * m : P * (m + 1)], rhs=hq[:].bitcast(E4M3X4), rhs_scale=hs[:],
                                 start=True, stop=True)
             p_sb = keep.tile([P, O], F32, name="p%d" % m)
-            if m == 0:
-                nc.vector.tensor_copy(p_sb[:], acc[:])
-            else:
-                nc.scalar.copy(p_sb[:], acc[:])
+            nc.vector.tensor_copy(p_sb[:], acc[:])
             res.append(p_sb)
-        for m in range(N // P):
-            nc.scalar.activation(pages["pa", m][:].indirect(o6[:]), res[m][:], COPY)
-            nc.vector.tensor_copy(pages["pb", m][:].indirect(o7[:]), res[m][:])
-        for m in range(N // P):
-            y = keep.tile([P, E], F32, name="y%d" % m)
-            nc.vector.tensor_tensor(y[:], pages["pa", m][:], pages["pb", m][:], ALU.add)
-            nc.sync.dma_start(out[P * m : P * (m + 1), :], y[:])
+        nc.scalar.activation(pages["pa", 0][:].indirect(o6[:]), res[0][:], COPY)
+        nc.vector.tensor_copy(pages["pb", 0][:].indirect(o7[:]), res[0][:])
+        nc.vector.tensor_copy(pages["pb", 1][:].indirect(o7[:, 0:4]), res[1][:, 0:64])
+        nc.scalar.activation(pages["pa", 1][:].indirect(o6[:]), res[1][:], COPY)
+        nc.scalar.activation(pages["pb", 1][:].indirect(o7[:, 4:8]), res[1][:, 64:128], COPY)
+        y0 = keep.tile([P, E], F32, name="y0")
+        nc.vector.tensor_tensor(y0[:], pages["pa", 0][:], pages["pb", 0][:], ALU.add)
+        nc.sync.dma_start(out[0:P, :], y0[:])
+        for h in range(2):
+            cols = slice(E // 2 * h, E // 2 * (h + 1))
+            y1 = keep.tile([P, E // 2], F32, name="y1_%d" % h)
+            nc.vector.tensor_tensor(y1[:], pages["pa", 1][:, cols], pages["pb", 1][:, cols], ALU.add)
+            nc.sync.dma_start(out[P : 2 * P, cols], y1[:])

@@ -43,7 +43,7 @@ def tile_list_ownsum_twow_one_owntwopages_kernel(
                 queue.dma_start(plane[QUAD * q : QUAD * q + PACK, :].bitcast(I32), rows[PACK * q : PACK * (q + 1), :])
 
         def load_staged(queue, scales, name):
-            staged = keep.tile([PACK, QUADS, R // 4], I32, name=name)
+            staged = keep.tile([PACK, QUADS, T // 4], I32, name=name)
             queue.dma_start(staged[:], scales[0].bitcast(I32).rearrange("(q r) n -> r q n", r=PACK))
             return staged
 
@@ -51,27 +51,31 @@ def tile_list_ownsum_twow_one_owntwopages_kernel(
             for q in range(QUADS):
                 nc.vector.tensor_copy(plane[QUAD * q : QUAD * q + PACK, :].bitcast(I32), staged[:, q, :])
 
-        def dealt_view(ap):
-            return ap.rearrange("p (m t) -> p t m", t=PACK)
+        def deal(copy, dst, src, first, run):
+            slots = dst.shape[1]
+            copy(dst.rearrange("p t (c i) -> p c t i", i=run),
+                 src.rearrange("p (c i t) -> p c t i", i=run, t=PACK)[:, :, first : first + slots, :])
 
-        x_plane = keep.tile([P, T], U8, name="x_plane", align_bytes=64)
-        nc.vector.memset(x_plane[:].bitcast(I32), 0)
         w_plane = keep.tile([P, R], U8, name="w_plane")
         nc.vector.memset(w_plane[:].bitcast(I32), 0)
+        x_plane = keep.tile([P, T], U8, name="x_plane", align_bytes=64)
+        nc.vector.memset(x_plane[:].bitcast(I32), 0)
+        w2_plane = keep.tile([P, R], U8, name="w2_plane")
+        nc.vector.memset(w2_plane[:].bitcast(I32), 0)
         wb_plane = keep.tile([P, N], U8, name="wb_plane", align_bytes=64)
         nc.vector.memset(wb_plane[:].bitcast(I32), 0)
 
         x_table = keep.tile([P, T], I32, name="x_table", align_bytes=64)
         w_raw = keep.tile([P, 2 * R], U8, name="w_raw")
+        x_staged = load_staged(nc.sync, xt_scales, "x_staged")
         o1 = load_list(offs, "o1")
-        w_staged = load_staged(nc.sync, w_scales, "w_staged")
-        load_plane(nc.scalar, x_plane, xt_scales)
+        load_plane(nc.scalar, w_plane, w_scales)
         nc.sync.dma_start(x_table[:], xt_words[0].rearrange("p n t -> p (n t)").bitcast(I32))
         nc.sync.dma_start(w_raw[:].bitcast(I32), w_words[0].bitcast(I32))
         o2 = load_list(offs2, "o2")
-        w2_staged = load_staged(nc.sync, w2_scales, "w2_staged")
         w2_raw = keep.tile([P, R], I32, name="w2_raw")
         nc.sync.dma_start(w2_raw[:], w2_words[0].rearrange("p n t -> p (n t)").bitcast(I32))
+        load_plane(nc.sync, w2_plane, w2_scales)
         o3 = load_list(offs3, "o3")
         o4 = load_list(offs4, "o4")
         o5 = load_list(offs5, "o5")
@@ -93,17 +97,19 @@ def tile_list_ownsum_twow_one_owntwopages_kernel(
 
         clear_board("pw", 0, "pw0")
         clear_board("pw", 1, "pw1")
+        clear_board("pw", 2, "pw2")
+        clear_board("pw", 3, "pw3")
 
-        w_first = keep.tile([P, 2 * P], U8, name="w_first", align_bytes=64)
-        nc.scalar.copy(w_first[:].bitcast(U16), dealt_view(w_raw[:].bitcast(U16))[:, 0, :])
+        w_first = keep.tile([P, 1, 2 * P], U8, name="w_first", align_bytes=64)
+        deal(nc.scalar.copy, w_first[:].bitcast(U16), w_raw[:].bitcast(U16), 0, 8)
         w_rest = keep.tile([P, PACK - 1, 2 * P], U8, name="w_rest", align_bytes=64)
-        nc.scalar.copy(w_rest[:].bitcast(U16), dealt_view(w_raw[:].bitcast(U16))[:, 1:, :])
-        spread_scales(w_staged, w_plane)
-        ws_first = keep.tile([P, P], U8, name="ws_first", align_bytes=64)
-        nc.vector.tensor_copy(ws_first[:], dealt_view(w_plane[:])[:, 0, :])
+        deal(nc.scalar.copy, w_rest[:].bitcast(U16), w_raw[:].bitcast(U16), 1, 8)
+        spread_scales(x_staged, x_plane)
         xs = keep.tile([P, J], U8, name="xs", align_bytes=64)
         nc.vector.tensor_copy(xs[:], x_plane[:].indirect(o1[:]))
-        xw = keep.tile([P, J], U32, name="xw", tag="x_plane", align_bytes=64)
+        ws_first = keep.tile([P, 1, P], U8, name="ws_first", align_bytes=64)
+        deal(nc.vector.tensor_copy, ws_first[:], w_plane[:], 0, 16)
+        xw = keep.tile([P, J], U32, name="xw", align_bytes=64)
         HALF = J // 2
         halves = [(slice(HALF * h, HALF * (h + 1)), slice(HALF // 16 * h, HALF // 16 * (h + 1))) for h in range(2)]
         for cols, offc in halves:
@@ -119,28 +125,24 @@ def tile_list_ownsum_twow_one_owntwopages_kernel(
             return res
 
         whole = slice(0, J)
-        a0 = [product("a0_%d" % h, w_first[:].bitcast(E2M1X4), ws_first[:], halves[h][0], "bank%d" % h) for h in range(2)]
+        a0 = [product("a0_%d" % h, w_first[:, 0, :].bitcast(E2M1X4), ws_first[:, 0, :], halves[h][0], "bank%d" % h) for h in range(2)]
         ws_rest = keep.tile([P, PACK - 1, P], U8, name="ws_rest", tag="ws_first", align_bytes=64)
-        nc.vector.tensor_copy(ws_rest[:], dealt_view(w_plane[:])[:, 1:, :])
+        deal(nc.vector.tensor_copy, ws_rest[:], w_plane[:], 1, 16)
         a = [None]
         for t in range(1, PACK):
             a.append(product("a%d" % t, w_rest[:, t - 1, :].bitcast(E2M1X4), ws_rest[:, t - 1, :], whole, "bank%d" % (1 + t)))
-        clear_board("pw", 2, "w_first")
-        clear_board("pw", 3, "ws_first")
         clear_board("pv", 0, "w_rest")
-        w2_plane = keep.tile([P, R], U8, name="w2_plane", tag="w_plane")
-        nc.vector.memset(w2_plane[:].bitcast(I32), 0)
-        spread_scales(w2_staged, w2_plane)
-        w2s_dealt = keep.tile([P, PACK, P], U8, name="w2s_dealt", align_bytes=64)
-        nc.vector.tensor_copy(w2s_dealt[:], dealt_view(w2_plane[:]))
-        w2_dealt = keep.tile([P, PACK, P], I32, name="w2_dealt", tag="a0_0", align_bytes=64)
-        nc.vector.tensor_copy(w2_dealt[:], dealt_view(w2_raw[:]))
+        w2s_dealt = keep.tile([P, PACK, P], U8, name="w2s_dealt", tag="w_first", align_bytes=64)
+        deal(nc.vector.tensor_copy, w2s_dealt[:], w2_plane[:], 0, 16)
+        w2_dealt = keep.tile([P, PACK, P], I32, name="w2_dealt", tag="ws_first", align_bytes=64)
+        deal(nc.vector.tensor_copy, w2_dealt[:], w2_raw[:], 0, 4)
         b = []
         for t in range(PACK):
             b.append(product("b%d" % t, w2_dealt[:, t, :].bitcast(E4M3X4), w2s_dealt[:, t, :], whole, "bank%d" % ((5 + t) % 8)))
-        clear_board("pv", 1, "w2s_dealt")
+        clear_board("pv", 1, "w_first")
 
         hid = keep.tile([P, O, PACK], BF16, name="hid", align_bytes=64)
+        diff = keep.tile([P, PACK, O], F32, name="diff")
         pg = {}
 
         def place_first(t):
@@ -157,14 +159,20 @@ def tile_list_ownsum_twow_one_owntwopages_kernel(
             pg[t] = keep.tile([P, C], F32, name="pg%d" % t)
             nc.vector.tensor_tensor(pg[t][:], pw[:], pv[:], ALU.add)
 
-        def fetch(t):
-            first = keep.tile([P, O], F32, name="first%d" % t)
-            nc.scalar.activation(first[:], pg[t][:].indirect(o4[:]), COPY, scale=sa_t[:, t : t + 1])
-            second = keep.tile([P, O], F32, name="second%d" % t)
-            nc.scalar.activation(second[:], pg[t][:].indirect(o5[:]), COPY, scale=sb_t[:, t : t + 1])
-            diff = keep.tile([P, O], F32, name="diff%d" % t)
-            nc.vector.tensor_tensor(diff[:], first[:], second[:], ALU.subtract)
-            nc.vector.scalar_tensor_tensor(hid[:, :, t], diff[:], -1.0, diff[:], ALU.mult, ALU.max)
+        first = {}
+
+        def fetch_first(t):
+            first[t] = keep.tile([P, O], F32, name="first%d" % t)
+            nc.scalar.activation(first[t][:], pg[t][:].indirect(o4[:]), COPY, scale=sa_t[:, t : t + 1])
+
+        def fetch_second(t, lo, hi):
+            second = keep.tile([P, hi - lo], F32, name="second%d_%d" % (t, lo))
+            nc.scalar.activation(second[:], pg[t][:].indirect(o5[:, lo // 16 : hi // 16]), COPY, scale=sb_t[:, t : t + 1])
+            nc.vector.tensor_tensor(diff[:, t, lo:hi], first[t][:, lo:hi], second[:], ALU.subtract)
+
+        def magnitude(t, lo, hi):
+            pair = diff[:, t : t + 2, lo:hi].rearrange("p t o -> p o t")
+            nc.vector.scalar_tensor_tensor(hid[:, lo:hi, t : t + 2], pair, -1.0, pair, ALU.mult, ALU.max)
 
         pages = {}
 
@@ -178,17 +186,27 @@ def tile_list_ownsum_twow_one_owntwopages_kernel(
         place_second(0)
         place_second(1)
         clear_pages(0, ("pw0", "b0"))
-        fetch(0)
+        fetch_first(0)
+        fetch_second(0, 0, O)
         place_second(2)
         clear_pages(1, ("pw1", "b1"))
-        fetch(1)
+        fetch_first(1)
         place_second(3)
-        fetch(2)
-        fetch(3)
-
+        fetch_second(1, 0, O)
+        magnitude(0, 0, O)
+        fetch_first(2)
+        fetch_second(2, 0, O)
+        fetch_first(3)
         hq = keep.tile([P, O], U32, name="hq", align_bytes=64)
         hs = keep.tile([P, O], U8, name="hs", align_bytes=64)
-        nc.vector.quantize_mx(out=hq[:].bitcast(E4M3X4), scales=hs[:], in_=hid[:].rearrange("p o t -> p (o t)"))
+        for lo in (0, O // 2):
+            fetch_second(3, lo, lo + O // 2)
+        for lo in (0, O // 2):
+            magnitude(2, lo, lo + O // 2)
+        for lo in (0, O // 2):
+            hi = lo + O // 2
+            nc.vector.quantize_mx(out=hq[:, lo:hi].bitcast(E4M3X4), scales=hs[:, lo:hi],
+                                  in_=hid[:, lo:hi, :].rearrange("p o t -> p (o t)"))
 
         res = []
         for m in range(N // P):

@@ -97,8 +97,6 @@ def tile_list_ownsum_twow_one_owntwopages_kernel(
 
         clear_board("pw", 0, "pw0")
         clear_board("pw", 1, "pw1")
-        clear_board("pw", 2, "pw2")
-        clear_board("pw", 3, "pw3")
 
         w_first = keep.tile([P, 1, 2 * P], U8, name="w_first", align_bytes=64)
         deal(nc.scalar.copy, w_first[:].bitcast(U16), w_raw[:].bitcast(U16), 0, 8)
@@ -131,15 +129,15 @@ def tile_list_ownsum_twow_one_owntwopages_kernel(
         a = [None]
         for t in range(1, PACK):
             a.append(product("a%d" % t, w_rest[:, t - 1, :].bitcast(E2M1X4), ws_rest[:, t - 1, :], whole, "bank%d" % (1 + t)))
-        clear_board("pv", 0, "w_rest")
-        w2s_dealt = keep.tile([P, PACK, P], U8, name="w2s_dealt", tag="w_first", align_bytes=64)
+        clear_board("pw", 2, "w_first")
+        clear_board("pw", 3, "w_rest")
+        w2s_dealt = keep.tile([P, PACK, P], U8, name="w2s_dealt", tag="ws_first", align_bytes=64)
         deal(nc.vector.tensor_copy, w2s_dealt[:], w2_plane[:], 0, 16)
-        w2_dealt = keep.tile([P, PACK, P], I32, name="w2_dealt", tag="ws_first", align_bytes=64)
+        w2_dealt = keep.tile([P, PACK, P], I32, name="w2_dealt", tag="a0_0", align_bytes=64)
         deal(nc.vector.tensor_copy, w2_dealt[:], w2_raw[:], 0, 4)
         b = []
         for t in range(PACK):
             b.append(product("b%d" % t, w2_dealt[:, t, :].bitcast(E4M3X4), w2s_dealt[:, t, :], whole, "bank%d" % ((5 + t) % 8)))
-        clear_board("pv", 1, "w_first")
 
         hid = keep.tile([P, O, PACK], BF16, name="hid", align_bytes=64)
         diff = keep.tile([P, PACK, O], F32, name="diff")
@@ -183,6 +181,8 @@ def tile_list_ownsum_twow_one_owntwopages_kernel(
 
         for t in range(PACK):
             place_first(t)
+        clear_board("pv", 0, "a0_1")
+        clear_board("pv", 1, "ws_first")
         place_second(0)
         place_second(1)
         clear_pages(0, ("pw0", "b0"))

from contextlib import ExitStack

import concourse.mybir as mybir

F32 = mybir.dt.float32
BF16 = mybir.dt.bfloat16
I32 = mybir.dt.int32
U32 = mybir.dt.uint32
U16 = mybir.dt.uint16
U8 = mybir.dt.uint8
E4M3X4 = mybir.dt.float8_e4m3fn_x4
E5M2X4 = mybir.dt.float8_e5m2_x4
E2M1X4 = mybir.dt.float4_e2m1fn_x4
COPY = mybir.ActivationFunctionType.Copy
ALU = mybir.AluOpType

K, T, J, R, C, O, N, E = 512, 1024, 256, 512, 512, 128, 256, 512
P = 128
PACK = 4
QUADS = 4
QUAD = 32
FLOPS = 2 * K * R * J * 2 + 2 * R * N * O


def tile_list_ownsum_twow_one_owntwopages_kernel(
    tc, xt_words, xt_scales, w_words, w_scales, w2_words, w2_scales, sa, sb, wb_words, wb_scales,
    offs, offs2, offs3, offs4, offs5, offs6, offs7, out,
):
    nc = tc.nc
    with ExitStack() as ctx:
        lists = ctx.enter_context(tc.tile_pool(name="lists", bufs=1))
        keep = ctx.enter_context(tc.tile_pool(name="keep", bufs=1))
        psum = ctx.enter_context(tc.psum_pool(name="psum", bufs=1))

        def load_list(src, name):
            t = lists.tile(list(src.shape), U16, name=name)
            nc.sync.dma_start(t[:], src)
            return t

        def load_plane(queue, plane, scales):
            rows = scales[0].bitcast(I32)
            for q in range(QUADS):
                queue.dma_start(plane[QUAD * q : QUAD * q + PACK, :].bitcast(I32), rows[PACK * q : PACK * (q + 1), :])

        def load_staged(queue, scales, name):
            staged = keep.tile([PACK, QUADS, T // 4], I32, name=name)
            queue.dma_start(staged[:], scales[0].bitcast(I32).rearrange("(q r) n -> r q n", r=PACK))
            return staged

        def spread_scales(staged, plane):
            for q in range(QUADS):
                nc.vector.tensor_copy(plane[QUAD * q : QUAD * q + PACK, :].bitcast(I32), staged[:, q, :])

        def deal(copy, dst, src, first, run):
            slots = dst.shape[1]
            copy(dst.rearrange("p t (c i) -> p c t i", i=run),
                 src.rearrange("p (c i t) -> p c t i", i=run, t=PACK)[:, :, first : first + slots, :])

        w_plane = keep.tile([P, R], U8, name="w_plane")
        nc.vector.memset(w_plane[:].bitcast(I32), 0)
        x_plane = keep.tile([P, T], U8, name="x_plane", align_bytes=64)
        nc.vector.memset(x_plane[:].bitcast(I32), 0)
        w2_plane = keep.tile([P, R], U8, name="w2_plane")
        nc.vector.memset(w2_plane[:].bitcast(I32), 0)
        wb_plane = keep.tile([P, N], U8, name="wb_plane", align_bytes=64)
        nc.vector.memset(wb_plane[:].bitcast(I32), 0)

        x_table = keep.tile([P, T], I32, name="x_table", align_bytes=64)
        w_raw = keep.tile([P, 2 * R], U8, name="w_raw")
        x_staged = load_staged(nc.sync, xt_scales, "x_staged")
        o1 = load_list(offs, "o1")
        load_plane(nc.scalar, w_plane, w_scales)
        nc.sync.dma_start(x_table[:], xt_words[0].rearrange("p n t -> p (n t)").bitcast(I32))
        nc.sync.dma_start(w_raw[:].bitcast(I32), w_words[0].bitcast(I32))
        o2 = load_list(offs2, "o2")
        w2_raw = keep.tile([P, R], I32, name="w2_raw")
        nc.sync.dma_start(w2_raw[:], w2_words[0].rearrange("p n t -> p (n t)").bitcast(I32))
        load_plane(nc.sync, w2_plane, w2_scales)
        o3 = load_list(offs3, "o3")
        o4 = load_list(offs4, "o4")
        o5 = load_list(offs5, "o5")
        sa_t = keep.tile([P, PACK], F32, name="sa_t")
        nc.sync.dma_start(sa_t[:], sa.rearrange("(p t) o -> p (t o)", t=PACK))
        sb_t = keep.tile([P, PACK], F32, name="sb_t")
        nc.sync.dma_start(sb_t[:], sb.rearrange("(p t) o -> p (t o)", t=PACK))
        wb_t = keep.tile([P, 2 * N], U8, name="wb_t", align_bytes=64)
        nc.sync.dma_start(wb_t[:].bitcast(I32), wb_words[0].bitcast(I32))
        load_plane(nc.sync, wb_plane, wb_scales)
        o6 = load_list(offs6, "o6")
        o7 = load_list(offs7, "o7")

        boards = {}

        def clear_board(side, half, tag):
            boards[side, half] = keep.tile([P, C], F32, name="%s%d" % (side, half), tag=tag, align_bytes=64)
            nc.vector.memset(boards[side, half][:], 0.0)

        clear_board("pw", 0, "pw0")
        clear_board("pw", 1, "pw1")

        w_first = keep.tile([P, 1, 2 * P], U8, name="w_first", align_bytes=64)
        deal(nc.scalar.copy, w_first[:].bitcast(U16), w_raw[:].bitcast(U16), 0, 8)
        w_rest = keep.tile([P, PACK - 1, 2 * P], U8, name="w_rest", align_bytes=64)
        deal(nc.scalar.copy, w_rest[:].bitcast(U16), w_raw[:].bitcast(U16), 1, 8)
        spread_scales(x_staged, x_plane)
        xs = keep.tile([P, J], U8, name="xs", align_bytes=64)
        nc.vector.tensor_copy(xs[:], x_plane[:].indirect(o1[:]))
        ws_first = keep.tile([P, 1, P], U8, name="ws_first", align_bytes=64)
        deal(nc.vector.tensor_copy, ws_first[:], w_plane[:], 0, 16)
        xw = keep.tile([P, J], U32, name="xw", align_bytes=64)
        HALF = J // 2
        halves = [(slice(HALF * h, HALF * (h + 1)), slice(HALF // 16 * h, HALF // 16 * (h + 1))) for h in range(2)]
        for cols, offc in halves:
            nc.vector.tensor_copy(xw[:, cols], x_table[:].bitcast(U32).indirect(o1[:, offc]))

        def product(name, words, scales, cols, tag):
            width = cols.stop - cols.start
            acc = psum.tile([P, width], F32, name=name + "_acc", tag=tag)
            nc.tensor.matmul_mx(out=acc[:], lhsT=words, lhsT_scale=scales, rhs=xw[:, cols].bitcast(E5M2X4), rhs_scale=xs[:, cols],
                                start=True, stop=True)
            res = keep.tile([P, width], F32, name=name, align_bytes=64)
            nc.vector.tensor_copy(res[:], acc[:])
            return res

        whole = slice(0, J)
        a0 = [product("a0_%d" % h, w_first[:, 0, :].bitcast(E2M1X4), ws_first[:, 0, :], halves[h][0], "bank%d" % h) for h in range(2)]
        ws_rest = keep.tile([P, PACK - 1, P], U8, name="ws_rest", tag="ws_first", align_bytes=64)
        deal(nc.vector.tensor_copy, ws_rest[:], w_plane[:], 1, 16)
        a = [None]
        for t in range(1, PACK):
            a.append(product("a%d" % t, w_rest[:, t - 1, :].bitcast(E2M1X4), ws_rest[:, t - 1, :], whole, "bank%d" % (1 + t)))
        clear_board("pw", 2, "w_first")
        clear_board("pw", 3, "w_rest")
        w2s_dealt = keep.tile([P, PACK, P], U8, name="w2s_dealt", tag="ws_first", align_bytes=64)
        deal(nc.vector.tensor_copy, w2s_dealt[:], w2_plane[:], 0, 16)
        w2_dealt = keep.tile([P, PACK, P], I32, name="w2_dealt", tag="a0_0", align_bytes=64)
        deal(nc.vector.tensor_copy, w2_dealt[:], w2_raw[:], 0, 4)
        b = []
        for t in range(PACK):
            b.append(product("b%d" % t, w2_dealt[:, t, :].bitcast(E4M3X4), w2s_dealt[:, t, :], whole, "bank%d" % ((5 + t) % 8)))

        hid = keep.tile([P, O, PACK], BF16, name="hid", align_bytes=64)
        diff = keep.tile([P, PACK, O], F32, name="diff")
        pg = {}

        def place_first(t):
            pw = boards["pw", t]
            if t == 0:
                for h in range(2):
                    nc.scalar.activation(pw[:].indirect(o2[:, halves[h][1]]), a0[h][:], COPY)
            else:
                nc.scalar.activation(pw[:].indirect(o2[:]), a[t][:], COPY)

        def place_second(t):
            pw, pv = boards["pw", t], boards["pv", t % 2]
            nc.scalar.activation(pv[:].indirect(o3[:]), b[t][:], COPY)
            pg[t] = keep.tile([P, C], F32, name="pg%d" % t)
            nc.vector.tensor_tensor(pg[t][:], pw[:], pv[:], ALU.add)

        first = {}

        def fetch_first(t):
            first[t] = keep.tile([P, O], F32, name="first%d" % t)
            nc.scalar.activation(first[t][:], pg[t][:].indirect(o4[:]), COPY, scale=sa_t[:, t : t + 1])

        def fetch_second(t, lo, hi):
            second = keep.tile([P, hi - lo], F32, name="second%d_%d" % (t, lo))
            nc.scalar.activation(second[:], pg[t][:].indirect(o5[:, lo // 16 : hi // 16]), COPY, scale=sb_t[:, t : t + 1])
            nc.vector.tensor_tensor(diff[:, t, lo:hi], first[t][:, lo:hi], second[:], ALU.subtract)

        def magnitude(t, lo, hi):
            pair = diff[:, t : t + 2, lo:hi].rearrange("p t o -> p o t")
            nc.vector.scalar_tensor_tensor(hid[:, lo:hi, t : t + 2], pair, -1.0, pair, ALU.mult, ALU.max)

        pages = {}

        def clear_pages(m, tags):
            for side, tag in zip(("pa", "pb"), tags):
                pages[side, m] = keep.tile([P, E], F32, name="%s%d" % (side, m), tag=tag, align_bytes=64)
                nc.vector.memset(pages[side, m][:], 0.0)

        for t in range(PACK):
            place_first(t)
        clear_board("pv", 0, "a0_1")
        clear_board("pv", 1, "ws_first")
        place_second(0)
        place_second(1)
        clear_pages(0, ("pw0", "b0"))
        fetch_first(0)
        fetch_second(0, 0, O)
        place_second(2)
        clear_pages(1, ("pw1", "b1"))
        fetch_first(1)
        place_second(3)
        fetch_second(1, 0, O)
        magnitude(0, 0, O)
        fetch_first(2)
        fetch_second(2, 0, O)
        fetch_first(3)
        hq = keep.tile([P, O], U32, name="hq", align_bytes=64)
        hs = keep.tile([P, O], U8, name="hs", align_bytes=64)
        for lo in (0, O // 2):
            fetch_second(3, lo, lo + O // 2)
        for lo in (0, O // 2):
            magnitude(2, lo, lo + O // 2)
        for lo in (0, O // 2):
            hi = lo + O // 2
            nc.vector.quantize_mx(out=hq[:, lo:hi].bitcast(E4M3X4), scales=hs[:, lo:hi],
                                  in_=hid[:, lo:hi, :].rearrange("p o t -> p (o t)"))

        res = []
        for m in range(N // P):
            acc = psum.tile([P, O], F32, name="p_acc%d" % m, tag="bank%d" % (1 + m))
            nc.tensor.matmul_mx(out=acc[:], lhsT=wb_t[:, 2 * P * m : 2 * P * (m + 1)].bitcast(E2M1X4),
                                lhsT_scale=wb_plane[:, P * m : P * (m + 1)], rhs=hq[:].bitcast(E4M3X4), rhs_scale=hs[:],
                                start=True, stop=True)
            p_sb = keep.tile([P, O], F32, name="p%d" % m)
            nc.vector.tensor_copy(p_sb[:], acc[:])
            res.append(p_sb)
        nc.scalar.activation(pages["pa", 0][:].indirect(o6[:]), res[0][:], COPY)
        nc.vector.tensor_copy(pages["pb", 0][:].indirect(o7[:]), res[0][:])
        nc.vector.tensor_copy(pages["pb", 1][:].indirect(o7[:, 0:4]), res[1][:, 0:64])
        nc.scalar.activation(pages["pa", 1][:].indirect(o6[:]), res[1][:], COPY)
        nc.scalar.activation(pages["pb", 1][:].indirect(o7[:, 4:8]), res[1][:, 64:128], COPY)
        y0 = keep.tile([P, E], F32, name="y0")
        nc.vector.tensor_tensor(y0[:], pages["pa", 0][:], pages["pb", 0][:], ALU.add)
        nc.sync.dma_start(out[0:P, :], y0[:])
        for h in range(2):
            cols = slice(E // 2 * h, E // 2 * (h + 1))
            y1 = keep.tile([P, E // 2], F32, name="y1_%d" % h)
            nc.vector.tensor_tensor(y1[:], pages["pa", 1][:, cols], pages["pb", 1][:, cols], ALU.add)
            nc.sync.dma_start(out[P : 2 * P, cols], y1[:])
